import numpy as np
import ml_dtypes

BF16 = ml_dtypes.bfloat16


def bf(x):
    return np.asarray(x, np.float32).astype(BF16)


def f32(x):
    return np.asarray(x, np.float32)


def f64(x):
    return np.asarray(x).astype(np.float64)


def striped(idx):
    return np.concatenate([l.reshape(-1, 16).T for l in idx])


def rows(idx, k):
    return np.tile(np.repeat(idx, 16, axis=0), (k // (16 * 8), 1))


def look(tab, idx):
    return np.take_along_axis(f64(tab), rows(idx, len(tab)), axis=1)


K, S, V, N, M = 512, 2048, 512, 512, 128


def setup_inputs():
    return {"tab": f32(np.random.standard_normal((K, S))), "w": bf(np.random.standard_normal((K, M)) / np.sqrt(K)), "b": f32(0.5 * np.random.standard_normal((M, 1))), "offs": striped(np.random.randint(0, S, (8, N)))}


def reference(tab, w, b, offs):
    idx = np.stack([g.T.reshape(-1) for g in np.split(offs, 8)])
    t = look(tab, idx)
    x = (t >= 0.25) * 0.5
    y = f64(w).T @ x
    return y + f64(b)

@@ -1,0 +1,39 @@
+import concourse.mybir as mybir
+
+P = 128
+THRESHOLD, LEVEL = 0.25, 0.5
+FLOPS = 2 * 512 * 128 * 512
+
+F32, BF16, U16 = mybir.dt.float32, mybir.dt.bfloat16, mybir.dt.uint16
+ALU = mybir.AluOpType
+
+
+def tile_lookup_deq_step_bias_kernel(tc, tab, w, b, offs, out):
+    nc = tc.nc
+    rows, table_columns = tab.shape
+    m, n = out.shape
+    blocks = rows // P
+    with (
+        tc.tile_pool(name="held", bufs=1) as held,
+        tc.psum_pool(name="psum", bufs=1) as psum,
+    ):
+        offsets = held.tile([P, n // 16], U16, name="offsets")
+        nc.sync.dma_start(offsets[:], offs)
+        weights = held.tile([P, blocks, m], BF16, name="weights")
+        nc.scalar.dma_start(weights[:], w.rearrange("(k p) m -> p k m", p=P))
+        bias = held.tile([m, 1], F32, name="bias")
+        nc.scalar.dma_start(bias[:], b)
+
+        product = psum.tile([m, n], F32, name="product")
+        for k in range(blocks):
+            window = held.tile([P, table_columns], F32, name=f"window{k}")
+            nc.sync.dma_start(window[:], tab[k * P:(k + 1) * P, :])
+            stepped = held.tile([P, n], F32, name=f"stepped{k}")
+            nc.vector.tensor_scalar(stepped[:], window[:].indirect(offsets[:]), THRESHOLD, LEVEL, ALU.is_ge, ALU.mult)
+            x = held.tile([P, n], BF16, name=f"x{k}")
+            nc.scalar.copy(x[:], stepped[:])
+            nc.tensor.matmul(product[:], weights[:, k, :], x[:], start=(k == 0), stop=(k == blocks - 1))
+
+        result = held.tile([m, n], F32, name="result")
+        nc.vector.tensor_scalar_add(result[:], product[:], bias[:])
+        nc.sync.dma_start(out, result[:])

@@ -6,6 +6,7 @@ FLOPS = 2 * 512 * 128 * 512
 
 F32, BF16, U16 = mybir.dt.float32, mybir.dt.bfloat16, mybir.dt.uint16
 ALU = mybir.AluOpType
+IDENTITY = mybir.ActivationFunctionType.Identity
 
 
 def tile_lookup_deq_step_bias_kernel(tc, tab, w, b, offs, out):
@@ -13,6 +14,7 @@ def tile_lookup_deq_step_bias_kernel(tc, tab, w, b, offs, out):
     rows, table_columns = tab.shape
     m, n = out.shape
     blocks = rows // P
+    half = n // 2
     with (
         tc.tile_pool(name="held", bufs=1) as held,
         tc.psum_pool(name="psum", bufs=1) as psum,
@@ -24,16 +26,21 @@ def tile_lookup_deq_step_bias_kernel(tc, tab, w, b, offs, out):
         bias = held.tile([m, 1], F32, name="bias")
         nc.scalar.dma_start(bias[:], b)
 
-        product = psum.tile([m, n], F32, name="product")
+        left = psum.tile([m, half], F32, name="left")
+        right = psum.tile([m, half], F32, name="right")
         for k in range(blocks):
             window = held.tile([P, table_columns], F32, name=f"window{k}")
             nc.sync.dma_start(window[:], tab[k * P:(k + 1) * P, :])
-            stepped = held.tile([P, n], F32, name=f"stepped{k}")
-            nc.vector.tensor_scalar(stepped[:], window[:].indirect(offsets[:]), THRESHOLD, LEVEL, ALU.is_ge, ALU.mult)
-            x = held.tile([P, n], BF16, name=f"x{k}")
-            nc.scalar.copy(x[:], stepped[:])
-            nc.tensor.matmul(product[:], weights[:, k, :], x[:], start=(k == 0), stop=(k == blocks - 1))
+            x = held.tile([P, n], F32, name=f"x{k}")
+            nc.vector.tensor_scalar(x[:], window[:].indirect(offsets[:]), THRESHOLD, LEVEL, ALU.is_ge, ALU.mult)
+            x_bf16 = x[:].bitcast(BF16)[:, 1::2]
+            first, last = k == 0, k == blocks - 1
+            nc.tensor.matmul(left[:], weights[:, k, :], x_bf16[:, :half], start=first, stop=last)
+            nc.tensor.matmul(right[:], weights[:, k, :], x_bf16[:, half:], start=first, stop=last)
 
-        result = held.tile([m, n], F32, name="result")
-        nc.vector.tensor_scalar_add(result[:], product[:], bias[:])
-        nc.sync.dma_start(out, result[:])
+        result_left = held.tile([m, half], F32, name="result_left")
+        nc.vector.tensor_scalar_add(result_left[:], left[:], bias[:])
+        nc.sync.dma_start(out[:, :half], result_left[:])
+        result_right = held.tile([m, half], F32, name="result_right")
+        nc.scalar.activation(result_right[:], right[:], IDENTITY, bias=bias[:])
+        nc.scalar.dma_start(out[:, half:], result_right[:])

import concourse.mybir as mybir

P = 128
THRESHOLD, LEVEL = 0.25, 0.5
FLOPS = 2 * 512 * 128 * 512

F32, BF16, U16 = mybir.dt.float32, mybir.dt.bfloat16, mybir.dt.uint16
ALU = mybir.AluOpType
IDENTITY = mybir.ActivationFunctionType.Identity


def tile_lookup_deq_step_bias_kernel(tc, tab, w, b, offs, out):
    nc = tc.nc
    rows, table_columns = tab.shape
    m, n = out.shape
    blocks = rows // P
    half = n // 2
    with (
        tc.tile_pool(name="held", bufs=1) as held,
        tc.psum_pool(name="psum", bufs=1) as psum,
    ):
        offsets = held.tile([P, n // 16], U16, name="offsets")
        nc.sync.dma_start(offsets[:], offs)
        weights = held.tile([P, blocks, m], BF16, name="weights")
        nc.scalar.dma_start(weights[:], w.rearrange("(k p) m -> p k m", p=P))
        bias = held.tile([m, 1], F32, name="bias")
        nc.scalar.dma_start(bias[:], b)

        left = psum.tile([m, half], F32, name="left")
        right = psum.tile([m, half], F32, name="right")
        for k in range(blocks):
            window = held.tile([P, table_columns], F32, name=f"window{k}")
            nc.sync.dma_start(window[:], tab[k * P:(k + 1) * P, :])
            x = held.tile([P, n], F32, name=f"x{k}")
            nc.vector.tensor_scalar(x[:], window[:].indirect(offsets[:]), THRESHOLD, LEVEL, ALU.is_ge, ALU.mult)
            x_bf16 = x[:].bitcast(BF16)[:, 1::2]
            first, last = k == 0, k == blocks - 1
            nc.tensor.matmul(left[:], weights[:, k, :], x_bf16[:, :half], start=first, stop=last)
            nc.tensor.matmul(right[:], weights[:, k, :], x_bf16[:, half:], start=first, stop=last)

        result_left = held.tile([m, half], F32, name="result_left")
        nc.vector.tensor_scalar_add(result_left[:], left[:], bias[:])
        nc.sync.dma_start(out[:, :half], result_left[:])
        result_right = held.tile([m, half], F32, name="result_right")
        nc.scalar.activation(result_right[:], right[:], IDENTITY, bias=bias[:])
        nc.scalar.dma_start(out[:, half:], result_right[:])
